import numpy as np, ml_dtypes
CORES = [14,30,46,142,158,174,270,286,302,398,414,430]
N = 12
KT, FB, TK = 1, 128, 64
def setup_inputs(rng):
    return {"x": rng.standard_normal((N, 128, KT * TK), dtype=np.float32).astype(ml_dtypes.bfloat16), "w": rng.standard_normal((N, 128, KT * N * FB), dtype=np.float32).astype(ml_dtypes.bfloat16)}
def setup_inputs_big(rng):
    d = setup_inputs(rng)
    for k in ("x", "w"): d[k] = (d[k].astype(np.float32) * 1024.0).astype(d[k].dtype)
    return d
def setup_inputs_small(rng):
    d = setup_inputs(rng)
    for k in ("x", "w"): d[k] = (d[k].astype(np.float32) * (1 / 1024.0)).astype(d[k].dtype)
    return d
def setup_inputs_apart(rng):
    d = setup_inputs(rng)
    f = (10.0 ** rng.permutation(np.linspace(-1.5, 1.5, N))).astype(np.float32).reshape(N, 1, 1)
    for k in ("x", "w"): d[k] = (d[k].astype(np.float32) * f).astype(d[k].dtype)
    return d
def reference(x, w):
    X, W = x.astype(np.float64), w.astype(np.float64)
    y = np.zeros((N, FB, N * TK))
    for j in range(N):
        for r in range(N):
            for t in range(KT):
                y[r][:, TK * j:TK * j + TK] += W[j][:, FB * (N * t + r):FB * (N * t + r) + FB].T @ X[j][:, TK * t:TK * t + TK]
    return {"y": y.astype(ml_dtypes.bfloat16 if x.dtype != np.float64 else np.float64)}

@@ -1,0 +1,174 @@
+from concourse.bass import DstId, RemoteDMATransfer
+
+N, FB, TK = 12, 128, 64
+HALF = N // 2
+W2 = 2 * TK
+TURNS = [[0, 1], [2, 3], [4]]
+
+SCRATCH = {
+    "xs": ("sbuf", [128, TK], "bfloat16"),
+    "ws": ("sbuf", [128, N * FB], "bfloat16"),
+    "stage": ("sbuf", [128, (HALF - 1) * W2], "bfloat16"),
+    "mix": ("sbuf", [128, HALF * W2], "bfloat16"),
+    "near": ("sbuf", [128, HALF * TK], "bfloat16"),
+    "far": ("sbuf", [128, HALF * TK], "bfloat16"),
+    "ps0": ("psum", [128, 512], "float32"),
+    "ps1": ("psum", [128, 512], "float32"),
+    "ps2": ("psum", [128, 512], "float32"),
+    "ps3": ("psum", [128, 512], "float32"),
+}
+SEMAPHORES = ["ld0", "ld1", "mm0", "mm1", "mm2", "mm3", "cp0", "cp1", "cp2", "cp3",
+              "pa0", "pa1", "pa2", "fa0", "fa1", "fa2", "nc", "sent", "done"]
+
+
+def _bits(mask):
+    return [b for b in range(16) if (mask >> b) & 1]
+
+
+def _runs(ids):
+    out = []
+    for i in sorted(ids):
+        if out and out[-1][1] == i:
+            out[-1][1] = i + 1
+        else:
+            out.append([i, i + 1])
+    return out
+
+
+def _plan(cores, topo):
+    n = len(cores)
+    host = [topo.host(c) for c in cores]
+    rack = [topo.rack(h) for h in host]
+    members = {}
+    for r in range(n):
+        members.setdefault(rack[r], []).append(r)
+    q = [members[rack[r]].index(r) for r in range(n)]
+    partner = [[d for d in range(n) if rack[d] != rack[r] and topo.may_write(cores[r], cores[d])
+                and topo.chip(cores[d]) == topo.chip(cores[r])][0] for r in range(n)]
+    order, sends = [], []
+    for r in range(n):
+        own = [d for d in members[rack[r]] if host[d] == host[r]]
+        oth = [d for d in members[rack[r]] if host[d] != host[r]]
+        i = own.index(r)
+        seq = [oth[(i + t) % len(oth)] for t in range(1, len(oth) + 1)]
+        seq += [own[(i + t) % len(own)] for t in range(1, len(own))]
+        order.append(seq)
+        calls = []
+        for turns in TURNS:
+            call = []
+            for m, t in enumerate(turns):
+                bits = _bits(topo.mask(cores[r], cores[seq[t]]))
+                share = len(bits) // len(turns)
+                call.append((t, seq[t], sum(1 << b for b in bits[m * share:(m + 1) * share]), share))
+            calls.append(call)
+        sends.append(calls)
+    need = [[0] * (HALF // 2) for _ in range(n)]
+    ready = [[-1] * (HALF // 2) for _ in range(n)]
+    for r in range(n):
+        for ci, call in enumerate(sends[r]):
+            for (t, d, mask, eng) in call:
+                need[d][q[r] // 2] += eng
+                ready[d][q[r] // 2] = max(ready[d][q[r] // 2], ci)
+    fwd = [sorted(range(HALF // 2), key=lambda k: (ready[r][k], k)) for r in range(n)]
+    return dict(members=members, rack=rack, q=q, partner=partner, order=order, sends=sends, need=need, fwd=fwd)
+
+
+def rank_program(g, core, T, topo):
+    me = T.rank_of(core)
+    if me is None:
+        return
+    cores = list(T.cores)
+    P = _plan(cores, topo)
+    q, partner, seq = P["q"], P["partner"], P["order"][me]
+    sem = T.sem
+    odd = q[me] % 2
+    my_col = (q[me] // 2) * 2 * W2 + odd * W2
+    ps = [T.ps0, T.ps1, T.ps2, T.ps3]
+    own_bank = len(TURNS)
+    queues = [g.sync, g.scalar]
+
+    first = [d for d in seq if topo.host(cores[d]) != topo.host(core)]
+    early = set(first) | set(partner[d] for d in first)
+    late = set(range(N)) - early
+    loads = [(T.xs[:, :], T.x[:, :], "ld0")]
+    for grp, name in ((early, "ld0"), (late, "ld1")):
+        for a, b in _runs(grp):
+            loads.append((T.ws[:, a * FB:b * FB], T.w[:, a * FB:b * FB], name))
+    count = {"ld0": 0, "ld1": 0}
+    for i, (dst, src, name) in enumerate(loads):
+        queues[i % 2].dma_start(dst, src).then_inc(sem[name], 16)
+        count[name] += 16
+
+    groups = [[seq[t] for t in turns] for turns in TURNS] + [[me]]
+    g.tensor.wait_ge(sem.ld0, count["ld0"])
+    have_late = False
+    for bank, readers in enumerate(groups):
+        tiles = []
+        for d in readers:
+            tiles += [partner[d], d] if odd else [d, partner[d]]
+        for i, t in enumerate(tiles):
+            if t in late and not have_late:
+                g.tensor.wait_ge(sem.ld1, count["ld1"])
+                have_late = True
+            g.tensor.matmul(ps[bank][:, i * TK:(i + 1) * TK], T.ws[:, t * FB:(t + 1) * FB], T.xs[:, :],
+                            True, True).then_inc(sem["mm%d" % bank], 1)
+
+    for bank, readers in enumerate(groups):
+        wdt = len(readers) * W2
+        g.vector.wait_ge(sem["mm%d" % bank], 2 * len(readers))
+        if bank == own_bank:
+            out = T.mix[:, my_col:my_col + W2]
+        else:
+            out = T.stage[:, TURNS[bank][0] * W2:TURNS[bank][0] * W2 + wdt]
+        g.vector.tensor_copy(out, ps[bank][:, 0:wdt]).then_inc(sem["cp%d" % bank], 1)
+
+    sent = 0
+    for ci, call in enumerate(P["sends"][me]):
+        g.wait_ge(sem["cp%d" % ci], 1)
+        trs = []
+        for (t, d, mask, eng) in call:
+            rid, pid = topo.addr(cores[d], core)
+            trs.append(RemoteDMATransfer(dst_ids=[DstId(rid=rid, pnc=pid)], dma_engine_mask=mask,
+                                         remote_sem=sem["pa%d" % (q[me] // 2)],
+                                         src=T.stage[:, t * W2:(t + 1) * W2], dst=T.mix[:, my_col:my_col + W2]))
+            sent += eng
+        g.remote_dma_fused(trs, local_sem=sem.sent)
+
+    pc = cores[partner[me]]
+    rid, pid = topo.addr(pc, core)
+    cmask = topo.mask(core, pc)
+    g.wait_ge(sem["cp%d" % own_bank], 1)
+    for k in P["fwd"][me]:
+        g.wait_ge(sem["pa%d" % k], P["need"][me][k])
+        g.remote_dma(out_ap=T.far[:, k * W2:(k + 1) * W2], in_ap=T.mix[:, k * 2 * W2 + TK:k * 2 * W2 + TK + W2],
+                     remote_sem=sem["fa%d" % k], local_sem=sem.sent, pid=pid, routing_id=rid, dma_engine_mask=cmask)
+        sent += len(_bits(cmask))
+
+    g.vector.wait_ge(sem["cp%d" % own_bank], 1)
+    for k in range(HALF // 2):
+        g.vector.wait_ge(sem["pa%d" % k], P["need"][me][k])
+    place = [(s // 2) * 4 + (3 if s % 2 else 0) for s in range(HALF)]
+    pieces = []
+    for s in range(HALF):
+        if pieces and place[s - 1] + 1 == place[s]:
+            pieces[-1][1] = s + 1
+        else:
+            pieces.append([s, s + 1])
+    for a, b in pieces:
+        g.vector.tensor_copy(T.near[:, a * TK:b * TK],
+                             T.mix[:, place[a] * TK:(place[a] + b - a) * TK]).then_inc(sem.nc, 1)
+
+    near0 = P["members"][P["rack"][me]][0] * TK
+    far0 = P["members"][P["rack"][partner[me]]][0] * TK
+    peng = len(_bits(topo.mask(pc, core)))
+    g.scalar.wait_ge(sem.nc, len(pieces))
+    g.scalar.dma_start(T.y[:, near0:near0 + HALF * TK], T.near[:, :]).then_inc(sem.done, 16)
+    stores = 16
+    for i, k in enumerate(P["fwd"][partner[me]]):
+        queues[i % 2].wait_ge(sem["fa%d" % k], peng)
+        queues[i % 2].dma_start(T.y[:, far0 + k * W2:far0 + (k + 1) * W2],
+                                T.far[:, k * W2:(k + 1) * W2]).then_inc(sem.done, 16)
+        stores += 16
+
+    g.wait_ge(sem.sent, sent)
+    g.wait_ge(sem.done, stores)

@@ -1,24 +1,21 @@
-from concourse.bass import DstId, RemoteDMATransfer
-
 N, FB, TK = 12, 128, 64
 HALF = N // 2
 W2 = 2 * TK
-TURNS = [[0, 1], [2, 3], [4]]
+NB = 5
 
 SCRATCH = {
     "xs": ("sbuf", [128, TK], "bfloat16"),
     "ws": ("sbuf", [128, N * FB], "bfloat16"),
-    "stage": ("sbuf", [128, (HALF - 1) * W2], "bfloat16"),
-    "mix": ("sbuf", [128, HALF * W2], "bfloat16"),
+    "stage": ("sbuf", [128, 5 * W2], "bfloat16"),
+    "mix": ("sbuf", [128, 7 * TK], "bfloat16"),
     "near": ("sbuf", [128, HALF * TK], "bfloat16"),
     "far": ("sbuf", [128, HALF * TK], "bfloat16"),
-    "ps0": ("psum", [128, 512], "float32"),
-    "ps1": ("psum", [128, 512], "float32"),
-    "ps2": ("psum", [128, 512], "float32"),
-    "ps3": ("psum", [128, 512], "float32"),
+    "sg": ("sbuf", [128, W2], "bfloat16"),
 }
-SEMAPHORES = ["ld0", "ld1", "mm0", "mm1", "mm2", "mm3", "cp0", "cp1", "cp2", "cp3",
-              "pa0", "pa1", "pa2", "fa0", "fa1", "fa2", "nc", "sent", "done"]
+for _b in range(NB):
+    SCRATCH["ps%d" % _b] = ("psum", [128, 512], "float32")
+SEMAPHORES = (["ld0", "ld1", "pa", "sa", "na", "da", "fp", "fs", "nc", "cpd", "cpo", "sent", "done"]
+              + ["mm%d" % _b for _b in range(NB)] + ["cp%d" % _b for _b in range(NB - 1)])
 
 
 def _bits(mask):
@@ -45,32 +42,24 @@ def _plan(cores, topo):
     q = [members[rack[r]].index(r) for r in range(n)]
     partner = [[d for d in range(n) if rack[d] != rack[r] and topo.may_write(cores[r], cores[d])
                 and topo.chip(cores[d]) == topo.chip(cores[r])][0] for r in range(n)]
-    order, sends = [], []
+    across, home = [], []
     for r in range(n):
         own = [d for d in members[rack[r]] if host[d] == host[r]]
         oth = [d for d in members[rack[r]] if host[d] != host[r]]
         i = own.index(r)
-        seq = [oth[(i + t) % len(oth)] for t in range(1, len(oth) + 1)]
-        seq += [own[(i + t) % len(own)] for t in range(1, len(own))]
-        order.append(seq)
-        calls = []
-        for turns in TURNS:
-            call = []
-            for m, t in enumerate(turns):
-                bits = _bits(topo.mask(cores[r], cores[seq[t]]))
-                share = len(bits) // len(turns)
-                call.append((t, seq[t], sum(1 << b for b in bits[m * share:(m + 1) * share]), share))
-            calls.append(call)
-        sends.append(calls)
-    need = [[0] * (HALF // 2) for _ in range(n)]
-    ready = [[-1] * (HALF // 2) for _ in range(n)]
-    for r in range(n):
-        for ci, call in enumerate(sends[r]):
-            for (t, d, mask, eng) in call:
-                need[d][q[r] // 2] += eng
-                ready[d][q[r] // 2] = max(ready[d][q[r] // 2], ci)
-    fwd = [sorted(range(HALF // 2), key=lambda k: (ready[r][k], k)) for r in range(n)]
-    return dict(members=members, rack=rack, q=q, partner=partner, order=order, sends=sends, need=need, fwd=fwd)
+        across.append([oth[(i + t) % len(oth)] for t in range(1, len(oth) + 1)])
+        home.append([own[(i + t) % len(own)] for t in range(1, len(own))])
+    lay = []
+    for f in range(n):
+        a, b, c = sorted(s for s in range(n) if f in across[s])
+        last = [s for s in (a, b, c) if across[s][-1] == f][0]
+        if last == a:
+            lay.append(dict(pair=(b, c), single=a, order=("pair", "single")))
+        elif last == c:
+            lay.append(dict(pair=(a, b), single=c, order=("pair", "single")))
+        else:
+            lay.append(dict(pair=(a, b), single=c, order=("single", "pair")))
+    return dict(members=members, rack=rack, q=q, partner=partner, across=across, home=home, lay=lay)
 
 
 def rank_program(g, core, T, topo):
@@ -79,16 +68,32 @@ def rank_program(g, core, T, topo):
         return
     cores = list(T.cores)
     P = _plan(cores, topo)
-    q, partner, seq = P["q"], P["partner"], P["order"][me]
+    q, partner, lay = P["q"], P["partner"], P["lay"]
+    across, home = P["across"][me], P["home"][me]
     sem = T.sem
-    odd = q[me] % 2
-    my_col = (q[me] // 2) * 2 * W2 + odd * W2
-    ps = [T.ps0, T.ps1, T.ps2, T.ps3]
-    own_bank = len(TURNS)
+    ps = [T["ps%d" % b] for b in range(NB)]
     queues = [g.sync, g.scalar]
+    sent = [0]
 
-    first = [d for d in seq if topo.host(cores[d]) != topo.host(core)]
-    early = set(first) | set(partner[d] for d in first)
+    def write(dst_rank, out_ap, in_ap, remote_sem):
+        d = cores[dst_rank]
+        rid, pid = topo.addr(d, core)
+        mask = topo.mask(core, d)
+        g.remote_dma(out_ap=out_ap, in_ap=in_ap, remote_sem=remote_sem, local_sem=sem.sent, pid=pid, routing_id=rid,
+                     dma_engine_mask=mask)
+        sent[0] += len(_bits(mask))
+
+    def engines(src_rank):
+        return len(_bits(topo.mask(cores[src_rank], core)))
+
+    def slot(p):
+        if me == lay[p]["pair"][0]:
+            return 0, True, sem.pa
+        if me == lay[p]["pair"][1]:
+            return 2, False, sem.pa
+        return 4, True, sem.sa
+
+    early = set(across) | set(partner[d] for d in across)
     late = set(range(N)) - early
     loads = [(T.xs[:, :], T.x[:, :], "ld0")]
     for grp, name in ((early, "ld0"), (late, "ld1")):
@@ -99,76 +104,83 @@ def rank_program(g, core, T, topo):
         queues[i % 2].dma_start(dst, src).then_inc(sem[name], 16)
         count[name] += 16
 
-    groups = [[seq[t] for t in turns] for turns in TURNS] + [[me]]
+    banks = [[p, partner[p]] if slot(p)[1] else [partner[p], p] for p in across]
+    banks.append([partner[p] for p in home] + list(home))
+    banks.append([partner[me], me])
     g.tensor.wait_ge(sem.ld0, count["ld0"])
-    have_late = False
-    for bank, readers in enumerate(groups):
-        tiles = []
-        for d in readers:
-            tiles += [partner[d], d] if odd else [d, partner[d]]
+    for bank, tiles in enumerate(banks):
+        if bank == len(across):
+            g.tensor.wait_ge(sem.ld1, count["ld1"])
         for i, t in enumerate(tiles):
-            if t in late and not have_late:
-                g.tensor.wait_ge(sem.ld1, count["ld1"])
-                have_late = True
             g.tensor.matmul(ps[bank][:, i * TK:(i + 1) * TK], T.ws[:, t * FB:(t + 1) * FB], T.xs[:, :],
                             True, True).then_inc(sem["mm%d" % bank], 1)
 
-    for bank, readers in enumerate(groups):
-        wdt = len(readers) * W2
-        g.vector.wait_ge(sem["mm%d" % bank], 2 * len(readers))
-        if bank == own_bank:
-            out = T.mix[:, my_col:my_col + W2]
+    col = 0
+    for bank in range(NB - 1):
+        wdt = len(banks[bank]) * TK
+        g.vector.wait_ge(sem["mm%d" % bank], len(banks[bank]))
+        g.vector.tensor_copy(T.stage[:, col:col + wdt], ps[bank][:, 0:wdt]).then_inc(sem["cp%d" % bank], 1)
+        col += wdt
+    g.vector.wait_ge(sem["mm%d" % (NB - 1)], 2)
+    g.vector.tensor_copy(T.mix[:, 6 * TK:7 * TK], ps[NB - 1][:, 0:TK]).then_inc(sem.cpd, 1)
+    g.vector.tensor_copy(T.near[:, q[me] * TK:(q[me] + 1) * TK], ps[NB - 1][:, TK:W2]).then_inc(sem.cpo, 1)
+
+    for t, p in enumerate(across):
+        blk, _, s = slot(p)
+        g.wait_ge(sem["cp%d" % t], 1)
+        write(p, T.mix[:, blk * TK:blk * TK + W2], T.stage[:, t * W2:(t + 1) * W2], s)
+
+    base = len(across) * W2
+    m0 = q[me] * TK
+    g.wait_ge(sem["cp%d" % len(across)], 1)
+    for j, p in enumerate(home):
+        write(partner[p], T.far[:, m0:m0 + TK], T.stage[:, base + j * TK:base + (j + 1) * TK], sem.da)
+    for j, p in enumerate(home):
+        k = len(home) + j
+        write(p, T.near[:, m0:m0 + TK], T.stage[:, base + k * TK:base + (k + 1) * TK], sem.na)
+
+    L = lay[me]
+    g.wait_ge(sem.cpd, 1)
+    for what in L["order"]:
+        if what == "pair":
+            g.wait_ge(sem.pa, engines(L["pair"][0]) + engines(L["pair"][1]))
+            c0 = q[L["pair"][0]] * TK
+            write(partner[me], T.far[:, c0:c0 + W2], T.mix[:, TK:TK + W2], sem.fp)
         else:
-            out = T.stage[:, TURNS[bank][0] * W2:TURNS[bank][0] * W2 + wdt]
-        g.vector.tensor_copy(out, ps[bank][:, 0:wdt]).then_inc(sem["cp%d" % bank], 1)
+            g.wait_ge(sem.sa, engines(L["single"]))
+            write(partner[me], T.sg[:, :], T.mix[:, 5 * TK:7 * TK], sem.fs)
 
-    sent = 0
-    for ci, call in enumerate(P["sends"][me]):
-        g.wait_ge(sem["cp%d" % ci], 1)
-        trs = []
-        for (t, d, mask, eng) in call:
-            rid, pid = topo.addr(cores[d], core)
-            trs.append(RemoteDMATransfer(dst_ids=[DstId(rid=rid, pnc=pid)], dma_engine_mask=mask,
-                                         remote_sem=sem["pa%d" % (q[me] // 2)],
-                                         src=T.stage[:, t * W2:(t + 1) * W2], dst=T.mix[:, my_col:my_col + W2]))
-            sent += eng
-        g.remote_dma_fused(trs, local_sem=sem.sent)
+    g.vector.wait_ge(sem.pa, engines(L["pair"][0]) + engines(L["pair"][1]))
+    g.vector.wait_ge(sem.sa, engines(L["single"]))
+    for s, blk in ((L["pair"][0], 0), (L["pair"][1], 3), (L["single"], 4)):
+        g.vector.tensor_copy(T.near[:, q[s] * TK:(q[s] + 1) * TK], T.mix[:, blk * TK:(blk + 1) * TK]).then_inc(sem.nc, 1)
 
-    pc = cores[partner[me]]
-    rid, pid = topo.addr(pc, core)
-    cmask = topo.mask(core, pc)
-    g.wait_ge(sem["cp%d" % own_bank], 1)
-    for k in P["fwd"][me]:
-        g.wait_ge(sem["pa%d" % k], P["need"][me][k])
-        g.remote_dma(out_ap=T.far[:, k * W2:(k + 1) * W2], in_ap=T.mix[:, k * 2 * W2 + TK:k * 2 * W2 + TK + W2],
-                     remote_sem=sem["fa%d" % k], local_sem=sem.sent, pid=pid, routing_id=rid, dma_engine_mask=cmask)
-        sent += len(_bits(cmask))
+    stores = [0]
 
-    g.vector.wait_ge(sem["cp%d" % own_bank], 1)
-    for k in range(HALF // 2):
-        g.vector.wait_ge(sem["pa%d" % k], P["need"][me][k])
-    place = [(s // 2) * 4 + (3 if s % 2 else 0) for s in range(HALF)]
-    pieces = []
-    for s in range(HALF):
-        if pieces and place[s - 1] + 1 == place[s]:
-            pieces[-1][1] = s + 1
-        else:
-            pieces.append([s, s + 1])
-    for a, b in pieces:
-        g.vector.tensor_copy(T.near[:, a * TK:b * TK],
-                             T.mix[:, place[a] * TK:(place[a] + b - a) * TK]).then_inc(sem.nc, 1)
+    def store(qu, c0, wdt, src):
+        qu.dma_start(T.y[:, c0:c0 + wdt], src).then_inc(sem.done, 16)
+        stores[0] += 16
 
     near0 = P["members"][P["rack"][me]][0] * TK
     far0 = P["members"][P["rack"][partner[me]]][0] * TK
-    peng = len(_bits(topo.mask(pc, core)))
-    g.scalar.wait_ge(sem.nc, len(pieces))
-    g.scalar.dma_start(T.y[:, near0:near0 + HALF * TK], T.near[:, :]).then_inc(sem.done, 16)
-    stores = 16
-    for i, k in enumerate(P["fwd"][partner[me]]):
-        queues[i % 2].wait_ge(sem["fa%d" % k], peng)
-        queues[i % 2].dma_start(T.y[:, far0 + k * W2:far0 + (k + 1) * W2],
-                                T.far[:, k * W2:(k + 1) * W2]).then_inc(sem.done, 16)
-        stores += 16
+    direct = [partner[p] for p in home]
+    g.sync.wait_ge(sem.da, sum(engines(s) for s in direct))
+    for a, b in _runs([q[s] for s in direct]):
+        store(g.sync, far0 + a * TK, (b - a) * TK, T.far[:, a * TK:b * TK])
+    g.scalar.wait_ge(sem.cpo, 1)
+    g.scalar.wait_ge(sem.na, sum(engines(s) for s in home))
+    g.scalar.wait_ge(sem.nc, 3)
+    store(g.scalar, near0, HALF * TK, T.near[:, :])
+    R = lay[partner[me]]
+    for what in R["order"]:
+        if what == "pair":
+            c0 = q[R["pair"][0]] * TK
+            g.sync.wait_ge(sem.fp, engines(partner[me]))
+            store(g.sync, far0 + c0, W2, T.far[:, c0:c0 + W2])
+        else:
+            for qu, s, blk in ((g.sync, R["single"], 0), (g.scalar, partner[me], 1)):
+                qu.wait_ge(sem.fs, engines(partner[me]))
+                store(qu, far0 + q[s] * TK, TK, T.sg[:, blk * TK:(blk + 1) * TK])
 
-    g.wait_ge(sem.sent, sent)
-    g.wait_ge(sem.done, stores)
+    g.wait_ge(sem.sent, sent[0])
+    g.wait_ge(sem.done, stores[0])

@@ -1,21 +1,20 @@
 N, FB, TK = 12, 128, 64
 HALF = N // 2
 W2 = 2 * TK
-NB = 5
+NB = 6
 
 SCRATCH = {
     "xs": ("sbuf", [128, TK], "bfloat16"),
     "ws": ("sbuf", [128, N * FB], "bfloat16"),
-    "stage": ("sbuf", [128, 5 * W2], "bfloat16"),
-    "mix": ("sbuf", [128, 7 * TK], "bfloat16"),
+    "stage": ("sbuf", [128, 11 * TK], "bfloat16"),
+    "mix": ("sbuf", [128, 6 * TK], "bfloat16"),
     "near": ("sbuf", [128, HALF * TK], "bfloat16"),
     "far": ("sbuf", [128, HALF * TK], "bfloat16"),
-    "sg": ("sbuf", [128, W2], "bfloat16"),
 }
 for _b in range(NB):
     SCRATCH["ps%d" % _b] = ("psum", [128, 512], "float32")
-SEMAPHORES = (["ld0", "ld1", "pa", "sa", "na", "da", "fp", "fs", "nc", "cpd", "cpo", "sent", "done"]
-              + ["mm%d" % _b for _b in range(NB)] + ["cp%d" % _b for _b in range(NB - 1)])
+SEMAPHORES = (["ld0", "ld1", "ld2", "pa", "sa", "na", "da", "fp", "fs", "nc", "sent", "done"]
+              + ["mm%d" % _b for _b in range(NB)] + ["cp%d" % _b for _b in range(NB)])
 
 
 def _bits(mask):
@@ -93,54 +92,58 @@ def rank_program(g, core, T, topo):
             return 2, False, sem.pa
         return 4, True, sem.sa
 
-    early = set(across) | set(partner[d] for d in across)
-    late = set(range(N)) - early
-    loads = [(T.xs[:, :], T.x[:, :], "ld0")]
-    for grp, name in ((early, "ld0"), (late, "ld1")):
+    need = [set([partner[me]]), set(across) | set(partner[d] for d in across)]
+    need.append(set(range(N)) - need[0] - need[1])
+    loads = [(T.xs[:, :], T.x[:, :], 0)]
+    for lv, grp in enumerate(need):
         for a, b in _runs(grp):
-            loads.append((T.ws[:, a * FB:b * FB], T.w[:, a * FB:b * FB], name))
-    count = {"ld0": 0, "ld1": 0}
-    for i, (dst, src, name) in enumerate(loads):
-        queues[i % 2].dma_start(dst, src).then_inc(sem[name], 16)
-        count[name] += 16
+            loads.append((T.ws[:, a * FB:b * FB], T.w[:, a * FB:b * FB], lv))
+    count = [0, 0, 0]
+    for i, (dst, src, lv) in enumerate(loads):
+        queues[i % 2].dma_start(dst, src).then_inc(sem["ld%d" % lv], 16)
+        count[lv] += 16
 
-    banks = [[p, partner[p]] if slot(p)[1] else [partner[p], p] for p in across]
+    banks = [[partner[me]]]
+    banks += [[p, partner[p]] if slot(p)[1] else [partner[p], p] for p in across]
     banks.append([partner[p] for p in home] + list(home))
-    banks.append([partner[me], me])
-    g.tensor.wait_ge(sem.ld0, count["ld0"])
+    banks.append([me])
+    level = [0] + [1] * len(across) + [2, 2]
+    have = -1
     for bank, tiles in enumerate(banks):
-        if bank == len(across):
-            g.tensor.wait_ge(sem.ld1, count["ld1"])
+        if level[bank] > have:
+            have = level[bank]
+            g.tensor.wait_ge(sem["ld%d" % have], count[have])
         for i, t in enumerate(tiles):
             g.tensor.matmul(ps[bank][:, i * TK:(i + 1) * TK], T.ws[:, t * FB:(t + 1) * FB], T.xs[:, :],
                             True, True).then_inc(sem["mm%d" % bank], 1)
 
-    col = 0
-    for bank in range(NB - 1):
-        wdt = len(banks[bank]) * TK
-        g.vector.wait_ge(sem["mm%d" % bank], len(banks[bank]))
-        g.vector.tensor_copy(T.stage[:, col:col + wdt], ps[bank][:, 0:wdt]).then_inc(sem["cp%d" % bank], 1)
+    m0 = q[me] * TK
+    col, at = 0, []
+    for bank, tiles in enumerate(banks):
+        wdt = len(tiles) * TK
+        g.vector.wait_ge(sem["mm%d" % bank], len(tiles))
+        out = T.near[:, m0:m0 + TK] if bank == NB - 1 else T.stage[:, col:col + wdt]
+        g.vector.tensor_copy(out, ps[bank][:, 0:wdt]).then_inc(sem["cp%d" % bank], 1)
+        at.append(col)
         col += wdt
-    g.vector.wait_ge(sem["mm%d" % (NB - 1)], 2)
-    g.vector.tensor_copy(T.mix[:, 6 * TK:7 * TK], ps[NB - 1][:, 0:TK]).then_inc(sem.cpd, 1)
-    g.vector.tensor_copy(T.near[:, q[me] * TK:(q[me] + 1) * TK], ps[NB - 1][:, TK:W2]).then_inc(sem.cpo, 1)
+
+    g.wait_ge(sem.cp0, 1)
+    write(partner[me], T.far[:, m0:m0 + TK], T.stage[:, at[0]:at[0] + TK], sem.da)
 
     for t, p in enumerate(across):
         blk, _, s = slot(p)
-        g.wait_ge(sem["cp%d" % t], 1)
-        write(p, T.mix[:, blk * TK:blk * TK + W2], T.stage[:, t * W2:(t + 1) * W2], s)
+        g.wait_ge(sem["cp%d" % (1 + t)], 1)
+        write(p, T.mix[:, blk * TK:blk * TK + W2], T.stage[:, at[1 + t]:at[1 + t] + W2], s)
 
-    base = len(across) * W2
-    m0 = q[me] * TK
-    g.wait_ge(sem["cp%d" % len(across)], 1)
+    bank = 1 + len(across)
+    g.wait_ge(sem["cp%d" % bank], 1)
     for j, p in enumerate(home):
-        write(partner[p], T.far[:, m0:m0 + TK], T.stage[:, base + j * TK:base + (j + 1) * TK], sem.da)
+        write(partner[p], T.far[:, m0:m0 + TK], T.stage[:, at[bank] + j * TK:at[bank] + (j + 1) * TK], sem.da)
     for j, p in enumerate(home):
         k = len(home) + j
-        write(p, T.near[:, m0:m0 + TK], T.stage[:, base + k * TK:base + (k + 1) * TK], sem.na)
+        write(p, T.near[:, m0:m0 + TK], T.stage[:, at[bank] + k * TK:at[bank] + (k + 1) * TK], sem.na)
 
     L = lay[me]
-    g.wait_ge(sem.cpd, 1)
     for what in L["order"]:
         if what == "pair":
             g.wait_ge(sem.pa, engines(L["pair"][0]) + engines(L["pair"][1]))
@@ -148,7 +151,8 @@ def rank_program(g, core, T, topo):
             write(partner[me], T.far[:, c0:c0 + W2], T.mix[:, TK:TK + W2], sem.fp)
         else:
             g.wait_ge(sem.sa, engines(L["single"]))
-            write(partner[me], T.sg[:, :], T.mix[:, 5 * TK:7 * TK], sem.fs)
+            c0 = q[L["single"]] * TK
+            write(partner[me], T.far[:, c0:c0 + TK], T.mix[:, 5 * TK:6 * TK], sem.fs)
 
     g.vector.wait_ge(sem.pa, engines(L["pair"][0]) + engines(L["pair"][1]))
     g.vector.wait_ge(sem.sa, engines(L["single"]))
@@ -157,30 +161,28 @@ def rank_program(g, core, T, topo):
 
     stores = [0]
 
-    def store(qu, c0, wdt, src):
-        qu.dma_start(T.y[:, c0:c0 + wdt], src).then_inc(sem.done, 16)
+    def store(qu, base, c0, wdt, buf):
+        qu.dma_start(T.y[:, base + c0:base + c0 + wdt], buf[:, c0:c0 + wdt]).then_inc(sem.done, 16)
         stores[0] += 16
 
     near0 = P["members"][P["rack"][me]][0] * TK
     far0 = P["members"][P["rack"][partner[me]]][0] * TK
-    direct = [partner[p] for p in home]
+    direct = [partner[me]] + [partner[p] for p in home]
     g.sync.wait_ge(sem.da, sum(engines(s) for s in direct))
     for a, b in _runs([q[s] for s in direct]):
-        store(g.sync, far0 + a * TK, (b - a) * TK, T.far[:, a * TK:b * TK])
-    g.scalar.wait_ge(sem.cpo, 1)
+        store(g.sync, far0, a * TK, (b - a) * TK, T.far)
+    g.scalar.wait_ge(sem["cp%d" % (NB - 1)], 1)
     g.scalar.wait_ge(sem.na, sum(engines(s) for s in home))
     g.scalar.wait_ge(sem.nc, 3)
-    store(g.scalar, near0, HALF * TK, T.near[:, :])
+    store(g.scalar, near0, 0, HALF * TK, T.near)
     R = lay[partner[me]]
-    for what in R["order"]:
+    for qu, what in zip((g.scalar, g.sync), R["order"]):
         if what == "pair":
-            c0 = q[R["pair"][0]] * TK
-            g.sync.wait_ge(sem.fp, engines(partner[me]))
-            store(g.sync, far0 + c0, W2, T.far[:, c0:c0 + W2])
+            qu.wait_ge(sem.fp, engines(partner[me]))
+            store(qu, far0, q[R["pair"][0]] * TK, W2, T.far)
         else:
-            for qu, s, blk in ((g.sync, R["single"], 0), (g.scalar, partner[me], 1)):
-                qu.wait_ge(sem.fs, engines(partner[me]))
-                store(qu, far0 + q[s] * TK, TK, T.sg[:, blk * TK:(blk + 1) * TK])
+            qu.wait_ge(sem.fs, engines(partner[me]))
+            store(qu, far0, q[R["single"]] * TK, TK, T.far)
 
     g.wait_ge(sem.sent, sent[0])
     g.wait_ge(sem.done, stores[0])

N, FB, TK = 12, 128, 64
HALF = N // 2
W2 = 2 * TK
NB = 6

SCRATCH = {
    "xs": ("sbuf", [128, TK], "bfloat16"),
    "ws": ("sbuf", [128, N * FB], "bfloat16"),
    "stage": ("sbuf", [128, 11 * TK], "bfloat16"),
    "mix": ("sbuf", [128, 6 * TK], "bfloat16"),
    "near": ("sbuf", [128, HALF * TK], "bfloat16"),
    "far": ("sbuf", [128, HALF * TK], "bfloat16"),
}
for _b in range(NB):
    SCRATCH["ps%d" % _b] = ("psum", [128, 512], "float32")
SEMAPHORES = (["ld0", "ld1", "ld2", "pa", "sa", "na", "da", "fp", "fs", "nc", "sent", "done"]
              + ["mm%d" % _b for _b in range(NB)] + ["cp%d" % _b for _b in range(NB)])


def _bits(mask):
    return [b for b in range(16) if (mask >> b) & 1]


def _runs(ids):
    out = []
    for i in sorted(ids):
        if out and out[-1][1] == i:
            out[-1][1] = i + 1
        else:
            out.append([i, i + 1])
    return out


def _plan(cores, topo):
    n = len(cores)
    host = [topo.host(c) for c in cores]
    rack = [topo.rack(h) for h in host]
    members = {}
    for r in range(n):
        members.setdefault(rack[r], []).append(r)
    q = [members[rack[r]].index(r) for r in range(n)]
    partner = [[d for d in range(n) if rack[d] != rack[r] and topo.may_write(cores[r], cores[d])
                and topo.chip(cores[d]) == topo.chip(cores[r])][0] for r in range(n)]
    across, home = [], []
    for r in range(n):
        own = [d for d in members[rack[r]] if host[d] == host[r]]
        oth = [d for d in members[rack[r]] if host[d] != host[r]]
        i = own.index(r)
        across.append([oth[(i + t) % len(oth)] for t in range(1, len(oth) + 1)])
        home.append([own[(i + t) % len(own)] for t in range(1, len(own))])
    lay = []
    for f in range(n):
        a, b, c = sorted(s for s in range(n) if f in across[s])
        last = [s for s in (a, b, c) if across[s][-1] == f][0]
        if last == a:
            lay.append(dict(pair=(b, c), single=a, order=("pair", "single")))
        elif last == c:
            lay.append(dict(pair=(a, b), single=c, order=("pair", "single")))
        else:
            lay.append(dict(pair=(a, b), single=c, order=("single", "pair")))
    return dict(members=members, rack=rack, q=q, partner=partner, across=across, home=home, lay=lay)


def rank_program(g, core, T, topo):
    me = T.rank_of(core)
    if me is None:
        return
    cores = list(T.cores)
    P = _plan(cores, topo)
    q, partner, lay = P["q"], P["partner"], P["lay"]
    across, home = P["across"][me], P["home"][me]
    sem = T.sem
    ps = [T["ps%d" % b] for b in range(NB)]
    queues = [g.sync, g.scalar]
    sent = [0]

    def write(dst_rank, out_ap, in_ap, remote_sem):
        d = cores[dst_rank]
        rid, pid = topo.addr(d, core)
        mask = topo.mask(core, d)
        g.remote_dma(out_ap=out_ap, in_ap=in_ap, remote_sem=remote_sem, local_sem=sem.sent, pid=pid, routing_id=rid,
                     dma_engine_mask=mask)
        sent[0] += len(_bits(mask))

    def engines(src_rank):
        return len(_bits(topo.mask(cores[src_rank], core)))

    def slot(p):
        if me == lay[p]["pair"][0]:
            return 0, True, sem.pa
        if me == lay[p]["pair"][1]:
            return 2, False, sem.pa
        return 4, True, sem.sa

    need = [set([partner[me]]), set(across) | set(partner[d] for d in across)]
    need.append(set(range(N)) - need[0] - need[1])
    loads = [(T.xs[:, :], T.x[:, :], 0)]
    for lv, grp in enumerate(need):
        for a, b in _runs(grp):
            loads.append((T.ws[:, a * FB:b * FB], T.w[:, a * FB:b * FB], lv))
    count = [0, 0, 0]
    for i, (dst, src, lv) in enumerate(loads):
        queues[i % 2].dma_start(dst, src).then_inc(sem["ld%d" % lv], 16)
        count[lv] += 16

    banks = [[partner[me]]]
    banks += [[p, partner[p]] if slot(p)[1] else [partner[p], p] for p in across]
    banks.append([partner[p] for p in home] + list(home))
    banks.append([me])
    level = [0] + [1] * len(across) + [2, 2]
    have = -1
    for bank, tiles in enumerate(banks):
        if level[bank] > have:
            have = level[bank]
            g.tensor.wait_ge(sem["ld%d" % have], count[have])
        for i, t in enumerate(tiles):
            g.tensor.matmul(ps[bank][:, i * TK:(i + 1) * TK], T.ws[:, t * FB:(t + 1) * FB], T.xs[:, :],
                            True, True).then_inc(sem["mm%d" % bank], 1)

    m0 = q[me] * TK
    col, at = 0, []
    for bank, tiles in enumerate(banks):
        wdt = len(tiles) * TK
        g.vector.wait_ge(sem["mm%d" % bank], len(tiles))
        out = T.near[:, m0:m0 + TK] if bank == NB - 1 else T.stage[:, col:col + wdt]
        g.vector.tensor_copy(out, ps[bank][:, 0:wdt]).then_inc(sem["cp%d" % bank], 1)
        at.append(col)
        col += wdt

    g.wait_ge(sem.cp0, 1)
    write(partner[me], T.far[:, m0:m0 + TK], T.stage[:, at[0]:at[0] + TK], sem.da)

    for t, p in enumerate(across):
        blk, _, s = slot(p)
        g.wait_ge(sem["cp%d" % (1 + t)], 1)
        write(p, T.mix[:, blk * TK:blk * TK + W2], T.stage[:, at[1 + t]:at[1 + t] + W2], s)

    bank = 1 + len(across)
    g.wait_ge(sem["cp%d" % bank], 1)
    for j, p in enumerate(home):
        write(partner[p], T.far[:, m0:m0 + TK], T.stage[:, at[bank] + j * TK:at[bank] + (j + 1) * TK], sem.da)
    for j, p in enumerate(home):
        k = len(home) + j
        write(p, T.near[:, m0:m0 + TK], T.stage[:, at[bank] + k * TK:at[bank] + (k + 1) * TK], sem.na)

    L = lay[me]
    for what in L["order"]:
        if what == "pair":
            g.wait_ge(sem.pa, engines(L["pair"][0]) + engines(L["pair"][1]))
            c0 = q[L["pair"][0]] * TK
            write(partner[me], T.far[:, c0:c0 + W2], T.mix[:, TK:TK + W2], sem.fp)
        else:
            g.wait_ge(sem.sa, engines(L["single"]))
            c0 = q[L["single"]] * TK
            write(partner[me], T.far[:, c0:c0 + TK], T.mix[:, 5 * TK:6 * TK], sem.fs)

    g.vector.wait_ge(sem.pa, engines(L["pair"][0]) + engines(L["pair"][1]))
    g.vector.wait_ge(sem.sa, engines(L["single"]))
    for s, blk in ((L["pair"][0], 0), (L["pair"][1], 3), (L["single"], 4)):
        g.vector.tensor_copy(T.near[:, q[s] * TK:(q[s] + 1) * TK], T.mix[:, blk * TK:(blk + 1) * TK]).then_inc(sem.nc, 1)

    stores = [0]

    def store(qu, base, c0, wdt, buf):
        qu.dma_start(T.y[:, base + c0:base + c0 + wdt], buf[:, c0:c0 + wdt]).then_inc(sem.done, 16)
        stores[0] += 16

    near0 = P["members"][P["rack"][me]][0] * TK
    far0 = P["members"][P["rack"][partner[me]]][0] * TK
    direct = [partner[me]] + [partner[p] for p in home]
    g.sync.wait_ge(sem.da, sum(engines(s) for s in direct))
    for a, b in _runs([q[s] for s in direct]):
        store(g.sync, far0, a * TK, (b - a) * TK, T.far)
    g.scalar.wait_ge(sem["cp%d" % (NB - 1)], 1)
    g.scalar.wait_ge(sem.na, sum(engines(s) for s in home))
    g.scalar.wait_ge(sem.nc, 3)
    store(g.scalar, near0, 0, HALF * TK, T.near)
    R = lay[partner[me]]
    for qu, what in zip((g.scalar, g.sync), R["order"]):
        if what == "pair":
            qu.wait_ge(sem.fp, engines(partner[me]))
            store(qu, far0, q[R["pair"][0]] * TK, W2, T.far)
        else:
            qu.wait_ge(sem.fs, engines(partner[me]))
            store(qu, far0, q[R["single"]] * TK, TK, T.far)

    g.wait_ge(sem.sent, sent[0])
    g.wait_ge(sem.done, stores[0])
